import numpy as np
import ml_dtypes


def mxq(x, axis, fmt="e4m3"):
    dtype, down = {"e4m3": (ml_dtypes.float8_e4m3fn, 7), "e5m2": (ml_dtypes.float8_e5m2, 14)}[fmt]
    v = np.moveaxis(np.asarray(x, np.float32).astype(ml_dtypes.bfloat16).astype(np.float64), axis, -1)
    blocks = v.reshape(v.shape[:-1] + (-1, 32))
    amax = np.abs(blocks).max(-1, keepdims=True)
    byte = np.maximum(np.where(amax > 0, np.frexp(amax)[1] - 1 + 127, 0) - down, 1)
    scale = np.exp2(byte - 127.0)
    codes = (blocks / scale).astype(np.float32).astype(dtype).astype(np.float64)
    return np.moveaxis((codes * scale).reshape(v.shape), -1, axis)


WIDE = False


def mx_kscale(k):
    if not WIDE:
        return np.ones(k)
    levels = np.array([10, -10, 5, -5, 0])
    if k % 512:
        return np.exp2(np.random.permutation(np.resize(levels, k // 32))).repeat(32)
    a = np.empty((k // 512, 16))
    for p in range(k // 512):
        a[p, :8] = np.random.permutation(np.resize(levels, 8))
        for g in range(8):
            far = levels[np.abs(levels - a[p, g]) >= 10]
            a[p, g + 8] = far[np.random.randint(len(far))]
    return np.exp2(a.ravel()).repeat(32)


def f64(x):
    return np.asarray(x).astype(np.float64)


def striped(idx):
    return np.tile(idx.reshape(-1, 16).T, (8, 1)).astype(np.uint16)


def unstriped(offs):
    return offs[:16].T.reshape(-1).astype(np.int64)


def pack_weight(w):
    k, n = w.shape
    w = f64(np.asarray(w, np.float32).astype(ml_dtypes.bfloat16)).reshape(k // 32, 32, n)
    amax = np.abs(w).max(1)
    byte = np.clip(np.where(amax > 0, np.frexp(amax)[1] - 1 + 127 - 7, 1), 1, 254)
    scaled = (w * np.exp2(127.0 - byte)[:, None, :]).reshape(k, n).astype(np.float32)
    words = np.ascontiguousarray(scaled.reshape(k // 512, 128, 4, n).transpose(0, 1, 3, 2)).astype(ml_dtypes.float8_e4m3fn).view(np.uint8)
    return words, np.ascontiguousarray(byte.astype(np.uint8).reshape(k // 512, 16, n))


def unpack_weight(words, scales):
    g, p, n, _ = words.shape
    vals = np.ascontiguousarray(words).view(ml_dtypes.float8_e4m3fn).astype(np.float64) * np.repeat(np.exp2(scales.astype(np.float64) - 127.0), 8, axis=1)[..., None]
    return vals.transpose(0, 1, 3, 2).reshape(g * 512, n)


K, T, S, N, U, D = 512, 2048, 512, 256, 1024, 4
P = 2 ** 7


def setup_inputs():
    n = np.random.standard_normal
    s = mx_kscale(K)[:, None]
    packed_xT = pack_weight(n((K, T)) * s)
    return {
        "x_words": packed_xT[0],
        "x_scales": packed_xT[1],
        "w1": (n((K, N)) / np.sqrt(K) / s).astype(np.float32),
        "free": (np.tile(np.random.uniform(0.3, 1.2, S), (P, 1))).astype(np.float32),
        "theta": (-np.random.uniform(0.8, 2.0, (N, 1))).astype(np.float32),
        "dem": (np.tile(np.random.uniform(0.5, 2.0, U), (P, 1))).astype(np.float32),
        "offs": striped(np.random.permutation(T)[:S]),
        "lka": striped(np.random.permutation(np.concatenate([np.arange(S), np.random.randint(0, S, U - S)]))),
        "lkb": striped(np.random.permutation(np.concatenate([np.arange(S), np.random.randint(0, S, U - S)]))),
    }


def reference(x_words, x_scales, w1, free, theta, dem, offs, lka, lkb):
    xq = unpack_weight(x_words, x_scales)[:, unstriped(offs)]
    y = mxq(f64(w1), 0, "e4m3").T @ xq
    load = 0.9 * (np.log(np.exp(y) + 1.0))
    time = f64(free)[:1] * (0.15 * (((load) ** 2) ** 2) + 1.0)
    rt = time[:, unstriped(lka)] + time[:, unstriped(lkb)]
    ut = f64(theta) * rt
    top = ut.reshape(len(ut), -1, D).max(axis=2)
    ex = np.exp(ut - np.repeat(top, D, axis=1))
    total = ex.reshape(len(ex), -1, D).sum(axis=2)
    share = ex / np.repeat(total, D, axis=1)
    return (share * f64(dem)[:1]) * np.sqrt(rt)

import math
from contextlib import ExitStack

import concourse.mybir as mybir
from concourse.masks import make_identity

K, T, S, N, U, D = 512, 2048, 512, 256, 1024, 4
P = 128
PACK = 4
TILES = N // P
HALF = S // 2
CHUNK = 512
TRIPS = U // D
SPARE = 32
EXP_CAP = 2.0 ** 40

FLOPS = 2 * K * N * S

F32 = mybir.dt.float32
BF16 = mybir.dt.bfloat16
I32 = mybir.dt.int32
U32 = mybir.dt.uint32
U16 = mybir.dt.uint16
U8 = mybir.dt.uint8
FP8X4 = mybir.dt.float8_e4m3fn_x4
ALU = mybir.AluOpType
ACT = mybir.ActivationFunctionType


def tile_picked_ybpr_flow_p_kernel(
    tc, x_words, x_scales, w1, free, theta, dem, offs, lka, lkb, out
):
    nc = tc.nc
    with ExitStack() as ctx:
        keep = ctx.enter_context(tc.tile_pool(name="keep", bufs=1))
        psum = ctx.enter_context(tc.psum_pool(name="psum", bufs=1))

        offs_sb = keep.tile([P, S // 16], U16, name="offs_sb")
        lka_sb = keep.tile([P, U // 16], U16, name="lka_sb")
        lkb_sb = keep.tile([P, U // 16], U16, name="lkb_sb")
        table_words = keep.tile([P, T], I32, name="table_words")
        table_scales = keep.tile([P, T], U8, name="table_scales")
        w_raw = keep.tile([P, PACK, N], F32, name="w_raw")
        theta_sb = keep.tile([P, TILES], F32, name="theta_sb")
        free_sb = keep.tile([P, S], F32, name="free_sb")
        dem_sb = keep.tile([P, U], F32, name="dem_sb")

        nc.gpsimd.memset(table_scales[:].bitcast(I32), 0)
        nc.sync.dma_start(offs_sb[:], offs)
        nc.sync.dma_start(w_raw[:], w1.rearrange("(p j) m -> p j m", j=PACK))
        for q in range(4):
            nc.sync.dma_start(
                table_scales[32 * q : 32 * q + 4, :].bitcast(I32), x_scales[0, 4 * q : 4 * q + 4, :].bitcast(I32)
            )
        nc.sync.dma_start(table_words[:], x_words[0].rearrange("p c r -> p (c r)").bitcast(I32))
        with nc.allow_non_contiguous_dma(reason="one theta to a partition and row tile"):
            nc.sync.dma_start(theta_sb[:], theta.rearrange("(t p) o -> p (t o)", p=P))
        nc.sync.dma_start(free_sb[:], free)
        nc.sync.dma_start(lka_sb[:], lka)
        nc.sync.dma_start(lkb_sb[:], lkb)
        nc.sync.dma_start(dem_sb[:], dem)

        times = [keep.tile([P, S + SPARE], F32, name=f"time{t}") for t in range(TILES)]
        for t in range(TILES):
            nc.gpsimd.memset(times[t][:, S:], 0.0)
        identity = keep.tile([P, P], F32, name="identity")
        make_identity(nc, identity[:])

        w_grouped = keep.tile([P, N, PACK], BF16, name="w_grouped", align_bytes=64)
        nc.scalar.activation(
            w_grouped[:].rearrange("p (c i) j -> p c j i", i=4),
            w_raw[:].rearrange("p j (c i) -> p c j i", i=4),
            ACT.Copy,
        )
        picked_scales = keep.tile([P, S], U8, name="picked_scales", align_bytes=64)
        nc.vector.tensor_copy(picked_scales[:], table_scales[:].indirect(offs_sb[:]))
        w_codes = keep.tile([P, N], U32, name="w_codes", align_bytes=64)
        w_scales = keep.tile([P, N], U8, name="w_scales", align_bytes=64)
        nc.vector.quantize_mx(
            out=w_codes[:].bitcast(FP8X4), scales=w_scales[:], in_=w_grouped[:].rearrange("p m j -> p (m j)")
        )

        picked_words = [keep.tile([P, HALF], U32, name=f"picked_words{h}", align_bytes=64) for h in range(2)]
        y = [[psum.tile([P, HALF], F32, name=f"y{t}{h}") for h in range(2)] for t in range(TILES)]
        grown = [[keep.tile([P, HALF], F32, name=f"grown{t}{h}") for h in range(2)] for t in range(TILES)]
        for h in range(2):
            nc.vector.tensor_copy(
                picked_words[h][:],
                table_words[:].bitcast(U32).indirect(offs_sb[:, h * HALF // 16 : (h + 1) * HALF // 16]),
            )
        for h in range(2):
            for t in range(TILES):
                nc.tensor.matmul_mx(
                    out=y[t][h][:],
                    lhsT=w_codes[:, t * P : (t + 1) * P].bitcast(FP8X4),
                    lhsT_scale=w_scales[:, t * P : (t + 1) * P],
                    rhs=picked_words[h][:].bitcast(FP8X4),
                    rhs_scale=picked_scales[:, h * HALF : (h + 1) * HALF],
                    start=True,
                    stop=True,
                )
                nc.scalar.activation(grown[t][h][:], y[t][h][:], ACT.Exp)

        sign = keep.tile([P, TILES], F32, name="sign")
        step = keep.tile([P, TILES], F32, name="step")
        size = keep.tile([P, TILES], F32, name="size")
        nc.vector.tensor_scalar(step[:], theta_sb[:], 0.0, 2.0, ALU.is_ge, ALU.mult)
        nc.vector.tensor_scalar(sign[:], step[:], -1.0, None, ALU.add)
        nc.vector.tensor_tensor(size[:], theta_sb[:], sign[:], ALU.mult)
        signed_free = [keep.tile([P, S], F32, name=f"signed_free{t}") for t in range(TILES)]

        capped = [[keep.tile([P, HALF], F32, name=f"capped{t}{h}") for h in range(2)] for t in range(TILES)]
        for h in range(2):
            for t in range(TILES):
                nc.vector.tensor_scalar(capped[t][h][:], grown[t][h][:], EXP_CAP, None, ALU.min)
        for t in range(TILES):
            nc.vector.tensor_scalar(signed_free[t][:], free_sb[:], sign[:, t : t + 1], None, ALU.mult)

        for t in range(TILES):
            logs = [keep.tile([P, HALF], F32, name=f"logs{t}{h}") for h in range(2)]
            soft = [keep.tile([P, HALF], F32, name=f"soft{t}{h}") for h in range(2)]
            second = [keep.tile([P, HALF], F32, name=f"second{t}{h}") for h in range(2)]
            fourth = [keep.tile([P, HALF], F32, name=f"fourth{t}{h}") for h in range(2)]
            for h in range(2):
                nc.scalar.activation(logs[h][:], capped[t][h][:], ACT.Ln, bias=1.0)
            for h in range(2):
                nc.vector.tensor_tensor(soft[h][:], y[t][h][:], logs[h][:], ALU.max)
            for h in range(2):
                nc.scalar.activation(second[h][:], soft[h][:], ACT.Square, scale=0.9)
            for h in range(2):
                nc.scalar.activation(fourth[h][:], second[h][:], ACT.Square, scale=math.sqrt(0.15))
            for h in range(2):
                cols = slice(h * HALF, (h + 1) * HALF)
                nc.vector.scalar_tensor_tensor(
                    times[t][:, cols], fourth[h][:], 1.0, signed_free[t][:, cols], ALU.add, ALU.mult
                )

        def wide(name, width):
            return [keep.tile([P, width], F32, name=f"{name}{t}") for t in range(TILES)]

        first_link, route, root, pair_top, top = wide("first_link", U), wide("route", U), wide("root", U), wide("pair_top", U // 2), wide("top", TRIPS)
        below, ex = wide("below", U), wide("ex", U)
        weight = [route[1], below[0]]
        total = [psum.tile([P, TRIPS], F32, name=f"total{t}") for t in range(TILES)]
        inverse_back = [psum.tile([P, TRIPS], F32, name=f"inverse_back{t}") for t in range(TILES)]
        total_sq, inverse, flow = wide("total_sq", TRIPS), wide("inverse", TRIPS), wide("flow", U)
        chunks = [slice(c, c + CHUNK) for c in range(0, U, CHUNK)]

        def by_trip(ap):
            return ap.rearrange("p (v d) -> p v d", d=D)

        def by_pair(ap):
            return ap.rearrange("p (v e) -> p v e", e=2)

        def spread(ap):
            return ap.unsqueeze(2).to_broadcast([P, ap.shape[1], D])

        for t in range(TILES):
            for c in chunks:
                nc.vector.tensor_copy(first_link[t][:, c], times[t][:].indirect(lka_sb[:, c.start // 16 : c.stop // 16]))
            for c in chunks:
                nc.vector.tensor_tensor(
                    route[t][:, c], times[t][:].indirect(lkb_sb[:, c.start // 16 : c.stop // 16]), first_link[t][:, c], ALU.add
                )
                nc.scalar.activation(root[t][:, c], route[t][:, c], ACT.Sqrt, scale=sign[:, t : t + 1])

        for t in range(TILES):
            nc.vector.tensor_tensor(by_pair(pair_top[t][:]), by_trip(route[t][:])[:, :, 0:2], by_trip(route[t][:])[:, :, 2:4], ALU.max)
        for t in range(TILES):
            nc.vector.tensor_tensor(top[t][:], by_pair(pair_top[t][:])[:, :, 0], by_pair(pair_top[t][:])[:, :, 1], ALU.max)
        for t in range(TILES):
            for c in chunks:
                nc.vector.tensor_tensor(
                    by_trip(below[t][:, c]), by_trip(route[t][:, c]), spread(top[t][:, c.start // D : c.stop // D]), ALU.subtract
                )
                nc.scalar.activation(ex[t][:, c], below[t][:, c], ACT.Exp, scale=size[:, t : t + 1])
        for t in range(TILES):
            nc.vector.tensor_tensor(weight[t][:], root[t][:], dem_sb[:], ALU.mult)
            for b in range(TRIPS // P):
                trips = slice(b * P, (b + 1) * P)
                for d in range(D):
                    nc.tensor.matmul(
                        total[t][:, trips], by_trip(ex[t][:])[:, trips, d], identity[:],
                        start=(d == 0), stop=(d == D - 1), is_transpose=True,
                    )
        for t in range(TILES):
            nc.scalar.activation(total_sq[t][:], total[t][:], ACT.Square)
            nc.scalar.activation(inverse[t][:], total_sq[t][:], ACT.Abs_reciprocal_sqrt)
            for b in range(TRIPS // P):
                trips = slice(b * P, (b + 1) * P)
                nc.tensor.transpose(inverse_back[t][:, trips], inverse[t][:, trips], identity[:])
        for t in range(TILES):
            nc.vector.tensor_tensor(flow[t][:], ex[t][:], weight[t][:], ALU.mult)
        for t in range(TILES):
            for c in chunks:
                result = keep.tile([P, CHUNK], F32, name=f"result{t}_{c.start}")
                nc.vector.tensor_tensor(
                    by_trip(result[:]), by_trip(flow[t][:, c]), spread(inverse_back[t][:, c.start // D : c.stop // D]), ALU.mult
                )
                nc.sync.dma_start(out[t * P : (t + 1) * P, c], result[:])
